import numpy as np, ml_dtypes
CORES = [44,45,46,47,172,173,174,175,300,301,302,303,428,429,430,431]
N = 16
import mx_ref
NC, ROOT = 128, 11
A = np.float32(0.0125)
BF = ml_dtypes.bfloat16
def cut(t, i, w=512):
    return t[:, w * i:w * i + w]
def tile(rs):
    return np.stack(rs, axis=2).reshape(128, -1).astype(BF)
def setup_inputs(rng):
    def f(*shape):
        return mx_ref.flush((rng.standard_normal(shape, dtype=np.float32) * np.exp2(rng.integers(-2, 3, shape[:-1] + (1,)))).astype(BF))
    return {"q": f(N, 128, 4 * NC), "k": f(N, 128, 4 * 512), "v": f(N, 128, 512)}
def setup_inputs_blocks(rng):
    d = setup_inputs(rng)
    for k in ("v",): d[k] = mx_ref.spread(d[k], rng, 4)
    for k in ("q", "k"): d[k] = mx_ref.spread(d[k], rng, 1)
    return d
def setup_inputs_wide(rng):
    d = setup_inputs(rng)
    for k in ("v",): d[k] = mx_ref.flush((d[k].astype(np.float32) * np.exp2(rng.integers(-8, 9, (N, 1, 1))).astype(np.float32)).astype(BF))
    return d
def setup_inputs_sharp(rng):
    d = setup_inputs(rng); v = d["q"].astype(np.float32).reshape(N, 128, -1, 4)
    d["q"] = mx_ref.flush((v * np.exp2(rng.integers(-2, 4, (N, 1, v.shape[2], 1))).astype(np.float32)).reshape(d["q"].shape).astype(BF))
    return d
def setup_inputs_offset(rng):
    d = setup_inputs(rng); v = d["k"].astype(np.float32).reshape(N, 128, -1, 4)
    d["k"] = mx_ref.flush((v + 12 * rng.standard_normal((1, 128, 1, 4), dtype=np.float32)).reshape(d["k"].shape).astype(BF))
    return d
def reference(q, k, v, own=None):
    ONE = mx_ref.quantize(np.ones((128, 512), BF)); Q = mx_ref.quantize(q[ROOT])
    S = [[mx_ref.matmul(mx_ref.quantize(cut(k[j], b)), Q) * A for b in range(4)] for j in range(N)]
    lo = np.stack([np.max(s, axis=(0, 1))[None] for s in S]); hi = np.broadcast_to(lo.max(axis=0) + 8, lo.shape).copy()
    c = lo if own is None else own["c"]
    p = np.stack([tile([np.exp(np.maximum(s - c[j], -20).astype(np.float64)).astype(np.float32) for s in S[j]]) for j in range(N)])
    use = p if own is None else own["p"]
    e = np.exp((c - c.max(axis=0)).astype(np.float64))[:, 0]; wlo = np.zeros((N, N, NC), np.float32); whi = np.ones((N, N, NC), np.float32); wlo[ROOT] = e * (1 - 4e-5); whi[ROOT] = e * (1 + 4e-5)
    w = np.zeros((N, N, NC), np.float32); w[ROOT] = e
    if own is not None: w = own["w"]
    num = den = 0
    for j in range(N):
        P = mx_ref.quantize(use[j])
        num = num + w[ROOT][j].astype(np.float64) * mx_ref.matmul(mx_ref.quantize(v[j]), P); den = den + w[ROOT][j].astype(np.float64) * mx_ref.matmul(ONE, P)
    o = np.full((N, 128, NC), np.nan, np.float32); o[ROOT] = (num / den).astype(np.float32)
    return {"c": c, "c__lo": lo, "c__hi": hi, "p": p, "w": w, "w__lo": wlo, "w__hi": whi, "o": o}

@@ -1,0 +1,343 @@
+import numpy as np
+from concourse.bass import DstId, RemoteDMATransfer
+from concourse.mybir import dt, AluOpType, AxisListType, ActivationFunctionType
+
+N = 16
+W = 129
+SL = 132
+A = float(np.float32(0.0125))
+
+SCRATCH = {
+    "qb": ("sbuf", [128, 512], "bfloat16"),
+    "qc": ("sbuf", [128, 128], "float8_e4m3fn_x4"),
+    "qs": ("sbuf", [128, 128], "uint8"),
+    "kb": ("sbuf", [128, 2048], "bfloat16"),
+    "kc": ("sbuf", [128, 512], "float8_e4m3fn_x4"),
+    "ks": ("sbuf", [128, 512], "uint8"),
+    "vb": ("sbuf", [128, 1024], "bfloat16"),
+    "vc": ("sbuf", [128, 256], "float8_e4m3fn_x4"),
+    "vs": ("sbuf", [128, 256], "uint8"),
+    "z": ("sbuf", [128, 512], "bfloat16"),
+    "one32": ("sbuf", [128, 32], "float32"),
+    "m2": ("sbuf", [128, 4], "float32"),
+    "cb": ("sbuf", [128, 32], "float32"),
+    "d0": ("sbuf", [128, 1024], "float32"),
+    "d1": ("sbuf", [128, 256], "float32"),
+    "d2": ("sbuf", [128, 1024], "float32"),
+    "pb": ("sbuf", [128, 512], "bfloat16"),
+    "pc": ("sbuf", [128, 128], "float8_e4m3fn_x4"),
+    "pl": ("sbuf", [128, 128], "uint8"),
+    "rt": ("sbuf", [128, SL], "float32"),
+    "ftl": ("sbuf", [128, SL], "float32"),
+    "fcl": ("sbuf", [128, 4], "float32"),
+    "land": ("sbuf", [128, N * SL], "float32"),
+    "CL": ("sbuf", [128, N], "float32"),
+    "sm": ("sbuf", [128, 8], "float32"),
+    "wp": ("sbuf", [128, N], "float32"),
+    "wT": ("sbuf", [128, 32], "float32"),
+    "wrow": ("sbuf", [128, 128], "float32"),
+    "acc": ("sbuf", [128, SL], "float32"),
+    "X": ("sbuf", [128, 128], "float32"),
+    "Z": ("sbuf", [128, 128], "float32"),
+    "ps": ("psum", [128, 3584], "float32"),
+}
+SEMAPHORES = (["ldq", "ldk", "ldv", "stc", "stp", "stw", "sto", "ms0", "ms", "ms2", "one", "qq", "qv", "qk", "qca", "qsa",
+               "st1", "st2", "r", "cm", "cb", "tr", "cp", "pe", "pq", "fm", "rt", "ls", "cea", "cla", "fca", "fta",
+               "e1", "e2", "e3", "e4", "ac", "f1", "f2", "f3", "f4", "f5", "wt", "rd", "xx"]
+              + ["s%d" % b for b in range(4)] + ["u%d" % b for b in range(4)] + ["sc%d" % b for b in range(4)]
+              + ["z%d" % b for b in range(4)] + ["t%d" % j for j in range(N)] + ["m%d" % j for j in range(N)])
+
+
+def _cnt(mask):
+    return bin(mask).count("1")
+
+
+def _pick(mask, lo, n):
+    bits = [b for b in range(16) if (mask >> b) & 1]
+    return sum(1 << b for b in bits[lo:lo + n])
+
+
+def rank_program(g, core, T, topo):
+    rank = T.rank_of(core)
+    if rank is None:
+        return
+    V, S, P, Y = g.vector, g.scalar, g.tensor, g.sync
+    AF, OP, AX = ActivationFunctionType, AluOpType, AxisListType
+    cores = list(T.cores)
+    rootc = cores[T.root]
+    is_root = core == rootc
+
+    def samechip(a, b):
+        return topo.host(a) == topo.host(b) and topo.chip(a) == topo.chip(b)
+
+    far = [c for c in cores if c != rootc and not topo.may_write(c, rootc)]
+    peers = [c for c in cores if c != rootc and samechip(c, rootc)]
+    mid = [c for c in cores if c != rootc and c not in far and c not in peers]
+    groups = [[c for c in mid if topo.host(c) == h] for h in sorted(set(topo.host(c) for c in mid))]
+    nf = len(far)
+    fwd = {far[i]: groups[i % len(groups)][i] for i in range(nf)}
+
+    tot, seen = {}, {}
+
+    def inc(ins, name, n=1):
+        ins.then_inc(T.sem[name], n)
+        tot[name] = tot.get(name, 0) + n
+
+    def expect(name, n):
+        tot[name] = tot.get(name, 0) + n
+
+    def wait(q, name):
+        q.wait_ge(T.sem[name], tot[name])
+        seen[name] = tot[name]
+
+    def upper(src, on_dst, off_dst):
+        on = topo.mask(src, on_dst)
+        up = on & ~topo.mask(src, off_dst)
+        return up if up else on
+
+    def q_plan(which):
+        rel = [grp[2 * which] for grp in groups]
+        plan = [(rootc, [([rel[k]], _pick(topo.mask(rootc, rel[k]), 4 * k, 4)) for k in range(len(groups))]),
+                (rootc, [(peers, upper(rootc, peers[0], rel[0]))])]
+        for k, r in enumerate(rel):
+            fs = far[2 * k:2 * k + 2]
+            plan.append((r, [([fs[i]], _pick(topo.mask(r, fs[i]), 4 * i, 4)) for i in range(len(fs))]))
+            others = [c for c in groups[k] if c != r]
+            plan.append((r, [(others, upper(r, others[0], fs[0]))]))
+        return plan
+
+    plans = [q_plan(0), q_plan(1)]
+    qsem = ["qca", "qsa"]
+    for which in range(2):
+        for snd, trs in plans[which]:
+            for dsts, m in trs:
+                if core in dsts:
+                    expect(qsem[which], _cnt(m))
+
+    def q_ap(which):
+        return T.qc[:].bitcast(dt.uint8) if which == 0 else T.qs[:]
+
+    def q_call(which, trs):
+        lst = []
+        for dsts, m in trs:
+            ids = []
+            for d in dsts:
+                rid, pid = topo.addr(d, core)
+                ids.append(DstId(rid=rid, pnc=pid))
+            lst.append(RemoteDMATransfer(dst_ids=ids, dma_engine_mask=m, remote_sem=T.sem[qsem[which]],
+                                         srcs=[q_ap(which)], dsts=[q_ap(which) for _ in dsts]))
+            expect("ls", _cnt(m))
+        g.remote_dma_fused(lst, local_sem=T.sem.ls)
+
+    def send(dst, out_ap, in_ap, sem):
+        rid, pid = topo.addr(dst, core)
+        m = topo.mask(core, dst)
+        g.remote_dma(out_ap=out_ap, in_ap=in_ap, remote_sem=T.sem[sem], local_sem=T.sem.ls, pid=pid, routing_id=rid,
+                     dma_engine_mask=m)
+        expect("ls", _cnt(m))
+
+    if is_root:
+        inc(Y.dma_start(T.qb[:], T.q[:]), "ldq", 16)
+        wait(Y, "ldq")
+    inc(Y.dma_start(T.kb[:], T.k[:]), "ldk", 16)
+    inc(Y.dma_start(T.vb[:, 0:512], T.v[:]), "ldv", 16)
+
+    inc(V.memset(T.z[:], 0.0), "ms0")
+    inc(V.memset(T.one32[:], 1.0), "ms")
+    inc(V.memset(T.d1[:], -20.0), "ms")
+    inc(V.memset(T.wrow[0:32, :], 0.0), "ms")
+    inc(V.memset(T.wT[:], 0.0), "ms")
+    wait(V, "ms")
+    wait(S, "ms0")
+    inc(S.activation(T.vb[:, 512:1024], T.z[:], AF.Exp), "one")
+    if is_root:
+        wait(V, "ldq")
+        inc(V.quantize_mx(T.qc[:], T.qs[:], T.qb[:]), "qq")
+    inc(V.memset(T.d0[:], -1e29), "ms2")
+    wait(V, "ms2")
+    wait(V, "one")
+    inc(V.quantize_mx(T.vc[:, 128:256], T.vs[:, 128:256], T.vb[:, 512:1024]), "qv")
+    wait(V, "ldv")
+    inc(V.quantize_mx(T.vc[:, 0:128], T.vs[:, 0:128], T.vb[:, 0:512]), "qv")
+    wait(V, "ldk")
+    inc(V.quantize_mx(T.kc[:], T.ks[:], T.kb[:]), "qk")
+    if not is_root:
+        wait(Y, "ms")
+        inc(Y.dma_start(T.w[:], T.wrow[0:N, :]), "stw", 16)
+
+    if is_root:
+        wait(g, "qq")
+        q_call(0, plans[0][0][1])
+        q_call(1, plans[1][0][1])
+        q_call(0, plans[0][1][1])
+        q_call(1, plans[1][1][1])
+    else:
+        for which in range(2):
+            mine = [trs for snd, trs in plans[which] if snd == core]
+            if mine:
+                wait(g, qsem[which])
+                for trs in mine:
+                    q_call(which, trs)
+
+    ps = T.ps
+    wait(P, "qk")
+    if is_root:
+        wait(P, "qq")
+    else:
+        wait(P, "qca")
+        wait(P, "qsa")
+    inc(P.matmul_mx(ps[:, 0:256], T.qc[:], T.qs[:], T.kc[:, 0:256], T.ks[:, 0:256], True, True), "st1")
+    inc(P.matmul_mx(ps[:, 512:768], T.qc[:], T.qs[:], T.kc[:, 256:512], T.ks[:, 256:512], True, True), "st2")
+    for b in range(4):
+        inc(P.matmul_mx(ps[:, 1024 + 512 * b:1152 + 512 * b], T.kc[:, 128 * b:128 * b + 128],
+                        T.ks[:, 128 * b:128 * b + 128], T.qc[:], T.qs[:], True, True), "s%d" % b)
+
+    wait(V, "st1")
+    inc(V.tensor_reduce(T.m2[:, 0:1], ps[:, 0:256], AX.X, OP.max), "r")
+    wait(V, "st2")
+    inc(V.tensor_reduce(T.m2[:, 1:2], ps[:, 512:768], AX.X, OP.max), "r")
+    wait(V, "r")
+    inc(V.tensor_scalar(T.m2[:, 2:3], T.m2[:, 0:1], T.m2[:, 1:2], A, OP.max, OP.mult), "cm")
+    wait(V, "cm")
+    inc(V.tensor_scalar(T.cb[:], T.one32[:], T.m2[:, 2:3], None, OP.mult), "cb")
+    wait(V, "cb")
+    for a in range(4):
+        inc(V.transpose(T.d1[0:32, 64 * a:64 * a + 64:2], T.cb[32 * a:32 * a + 32, :]), "tr")
+    wait(V, "tr")
+    inc(V.tensor_copy(T.d1[32:64, 0:256:2], T.d1[0:32, 0:256:2]), "cp")
+    wait(V, "cp")
+    inc(V.tensor_copy(T.d1[64:128, 0:256:2], T.d1[0:64, 0:256:2]), "cp")
+    wait(V, "cp")
+
+    wait(S, "ms2")
+    for b in range(4):
+        wait(S, "s%d" % b)
+        inc(S.activation(T.d0[:, 256 * b + 1:256 * b + 256:2], ps[:, 1024 + 512 * b:1152 + 512 * b], AF.Copy, scale=A),
+            "u%d" % b)
+    for b in range(4):
+        wait(V, "u%d" % b)
+        inc(V.tensor_tensor_scan(T.d2[:, 256 * b:256 * b + 256], T.d0[:, 256 * b:256 * b + 256], T.d1[:], 0.0,
+                                 OP.subtract, OP.max), "sc%d" % b)
+    for b in range(4):
+        wait(S, "sc%d" % b)
+        inc(S.activation(T.pb[:, b:512:4], T.d2[:, 256 * b + 1:256 * b + 256:2], AF.Exp), "pe")
+    wait(V, "pe")
+    inc(V.quantize_mx(T.pc[:], T.pl[:], T.pb[:]), "pq")
+
+    wait(P, "pq")
+    wait(P, "qv")
+    inc(P.matmul_mx(ps[:, 3072:3202], T.pc[:], T.pl[:], T.vc[:, 0:130], T.vs[:, 0:130], True, True), "fm")
+    wait(V, "fm")
+    own = T.land[:, SL * rank:SL * rank + W] if is_root else T.rt[:, 0:W]
+    inc(V.tensor_copy(own, ps[:, 3072:3072 + W]), "rt")
+
+    wait(Y, "cb")
+    inc(Y.dma_start(T.c[:], T.cb[:, 0:1]), "stc", 16)
+    wait(Y, "pe")
+    inc(Y.dma_start(T.p[:], T.pb[:]), "stp", 16)
+
+    if not is_root:
+        slot = T.land[:, SL * rank:SL * rank + W]
+        if core in far:
+            wait(g, "cb")
+            send(fwd[core], T.fcl[:, 0:1], T.cb[:, 0:1], "fca")
+            wait(g, "rt")
+            send(fwd[core], T.ftl[:, 0:W], T.rt[:, 0:W], "fta")
+        else:
+            wait(g, "cb")
+            send(rootc, T.CL[:, rank:rank + 1], T.cb[:, 0:1], "cea")
+            wait(g, "rt")
+            send(rootc, slot, T.rt[:, 0:W], "t%d" % rank)
+            for f in far:
+                if fwd[f] == core:
+                    j = T.rank_of(f)
+                    expect("fca", _cnt(topo.mask(f, core)))
+                    expect("fta", _cnt(topo.mask(f, core)))
+                    wait(g, "fca")
+                    send(rootc, T.CL[:, j:j + 1], T.fcl[:, 0:1], "cla")
+                    wait(g, "fta")
+                    send(rootc, T.land[:, SL * j:SL * j + W], T.ftl[:, 0:W], "t%d" % j)
+
+    if is_root:
+        for c in peers + mid:
+            expect("cea", _cnt(topo.mask(c, rootc)))
+            expect("t%d" % T.rank_of(c), _cnt(topo.mask(c, rootc)))
+        for f in far:
+            expect("cla", _cnt(topo.mask(fwd[f], rootc)))
+            expect("t%d" % T.rank_of(f), _cnt(topo.mask(fwd[f], rootc)))
+        sm, acc = T.sm, T.acc[:, 0:W]
+
+        def slot_of(j):
+            return T.land[:, SL * j:SL * j + W]
+
+        wait(V, "cea")
+        inc(V.tensor_copy(T.CL[:, rank:rank + 1], T.cb[:, 0:1]), "e1")
+        wait(V, "e1")
+        inc(V.tensor_reduce(sm[:, 0:1], T.CL[:, nf:N], AX.X, OP.max), "e2")
+        wait(V, "e2")
+        inc(V.tensor_scalar(sm[:, 1:2], sm[:, 0:1], -1.0, None, OP.mult), "e3")
+        wait(S, "cea")
+        wait(S, "e1")
+        wait(S, "e3")
+        inc(S.activation(T.wp[:, nf:N], T.CL[:, nf:N], AF.Exp, bias=sm[:, 1:2]), "e4")
+        wait(S, "e4")
+        order = [rank] + [T.rank_of(c) for c in peers]
+        for x in (0, 2, 1, 3):
+            order += [T.rank_of(grp[x]) for grp in groups]
+        for j in order:
+            wait(S, "rt" if j == rank else "t%d" % j)
+            inc(S.activation(slot_of(j), slot_of(j), AF.Copy, scale=T.wp[:, j:j + 1]), "m%d" % j)
+        for i, j in enumerate(order):
+            wait(V, "m%d" % j)
+            if i == 1:
+                inc(V.tensor_tensor(acc, slot_of(order[0]), slot_of(j), OP.add), "ac")
+            elif i > 1:
+                wait(V, "ac")
+                inc(V.tensor_tensor(acc, acc, slot_of(j), OP.add), "ac")
+
+        wait(V, "cla")
+        inc(V.tensor_reduce(sm[:, 2:3], T.CL[:, 0:nf], AX.X, OP.max), "f1")
+        wait(V, "f1")
+        inc(V.tensor_scalar(sm[:, 3:4], sm[:, 2:3], sm[:, 0:1], -1.0, OP.max, OP.mult), "f2")
+        wait(S, "cla")
+        wait(S, "f2")
+        inc(S.activation(sm[:, 4:5], sm[:, 0:1], AF.Exp, bias=sm[:, 3:4]), "f3")
+        inc(S.activation(T.wT[:, 0:nf], T.CL[:, 0:nf], AF.Exp, bias=sm[:, 3:4]), "f4")
+        wait(V, "f3")
+        wait(V, "ac")
+        inc(V.tensor_scalar(acc, acc, sm[:, 4:5], None, OP.mult), "ac")
+        wait(V, "e4")
+        inc(V.tensor_scalar(T.wT[:, nf:N], T.wp[:, nf:N], sm[:, 4:5], None, OP.mult), "f5")
+        wait(V, "f4")
+        wait(V, "f5")
+        for a in range(4):
+            inc(V.transpose(T.wrow[0:32, 32 * a:32 * a + 32], T.wT[32 * a:32 * a + 32, :]), "wt")
+        wait(Y, "wt")
+        inc(Y.dma_start(T.w[:], T.wrow[0:N, :]), "stw", 16)
+
+        wait(S, "f4")
+        for j in range(nf):
+            wait(S, "t%d" % j)
+            inc(S.activation(slot_of(j), slot_of(j), AF.Copy, scale=T.wT[:, j:j + 1]), "m%d" % j)
+        for j in range(nf):
+            wait(V, "m%d" % j)
+            wait(V, "ac")
+            inc(V.tensor_tensor(acc, acc, slot_of(j), OP.add), "ac")
+
+        wait(V, "ac")
+        inc(V.reciprocal(sm[:, 5:6], T.acc[:, 128:129]), "rd")
+        wait(V, "rd")
+        inc(V.tensor_scalar(T.X[:], T.acc[:, 0:128], sm[:, 5:6], None, OP.mult), "xx")
+        wait(V, "xx")
+        for b in range(4):
+            for a in range(4):
+                inc(V.transpose(T.Z[32 * b:32 * b + 32, 32 * a:32 * a + 32], T.X[32 * a:32 * a + 32, 32 * b:32 * b + 32]),
+                    "z%d" % b)
+        for b in range(4):
+            q = Y if b % 2 == 0 else S
+            wait(q, "z%d" % b)
+            inc(q.dma_start(T.o[32 * b:32 * b + 32, :], T.Z[32 * b:32 * b + 32, :]), "sto", 16)
+
+    for name in sorted(tot):
+        if seen.get(name, 0) < tot[name]:
+            wait(g, name)

@@ -17,7 +17,6 @@ SCRATCH = {
     "vb": ("sbuf", [128, 1024], "bfloat16"),
     "vc": ("sbuf", [128, 256], "float8_e4m3fn_x4"),
     "vs": ("sbuf", [128, 256], "uint8"),
-    "z": ("sbuf", [128, 512], "bfloat16"),
     "one32": ("sbuf", [128, 32], "float32"),
     "m2": ("sbuf", [128, 4], "float32"),
     "cb": ("sbuf", [128, 32], "float32"),
@@ -28,21 +27,23 @@ SCRATCH = {
     "pc": ("sbuf", [128, 128], "float8_e4m3fn_x4"),
     "pl": ("sbuf", [128, 128], "uint8"),
     "rt": ("sbuf", [128, SL], "float32"),
-    "ftl": ("sbuf", [128, SL], "float32"),
-    "fcl": ("sbuf", [128, 4], "float32"),
     "land": ("sbuf", [128, N * SL], "float32"),
     "CL": ("sbuf", [128, N], "float32"),
-    "sm": ("sbuf", [128, 8], "float32"),
+    "GT": ("sbuf", [128, 16], "float32"),
+    "wg": ("sbuf", [128, 16], "float32"),
+    "sm": ("sbuf", [128, 16], "float32"),
     "wp": ("sbuf", [128, N], "float32"),
     "wT": ("sbuf", [128, 32], "float32"),
     "wrow": ("sbuf", [128, 128], "float32"),
     "acc": ("sbuf", [128, SL], "float32"),
     "X": ("sbuf", [128, 128], "float32"),
+    "X2": ("sbuf", [128, 128], "float32"),
     "Z": ("sbuf", [128, 128], "float32"),
     "ps": ("psum", [128, 3584], "float32"),
 }
-SEMAPHORES = (["ldq", "ldk", "ldv", "stc", "stp", "stw", "sto", "ms0", "ms", "ms2", "one", "qq", "qv", "qk", "qca", "qsa",
-               "st1", "st2", "r", "cm", "cb", "tr", "cp", "pe", "pq", "fm", "rt", "ls", "cea", "cla", "fca", "fta",
+SEMAPHORES = (["ldq", "ldk", "ldv", "stc", "stp", "stw", "sto", "ms0", "ms", "ms2", "one", "w1", "qo", "qoa", "qq", "qv",
+               "qk", "qca", "qsa",
+               "st1", "st2", "r", "cm", "cb", "tr", "cp", "pe", "pq", "fm", "rt", "ls", "cea", "cla", "xt",
                "e1", "e2", "e3", "e4", "ac", "f1", "f2", "f3", "f4", "f5", "wt", "rd", "xx"]
               + ["s%d" % b for b in range(4)] + ["u%d" % b for b in range(4)] + ["sc%d" % b for b in range(4)]
               + ["z%d" % b for b in range(4)] + ["t%d" % j for j in range(N)] + ["m%d" % j for j in range(N)])
@@ -75,7 +76,19 @@ def rank_program(g, core, T, topo):
     mid = [c for c in cores if c != rootc and c not in far and c not in peers]
     groups = [[c for c in mid if topo.host(c) == h] for h in sorted(set(topo.host(c) for c in mid))]
     nf = len(far)
-    fwd = {far[i]: groups[i % len(groups)][i] for i in range(nf)}
+    ng = len(groups)
+    gath = [grp[-1] for grp in groups]
+    farm = [[far[i] for i in range(nf) if i % ng == k] for k in range(ng)]
+    others = [farm[k] + groups[k][:-1] for k in range(ng)]
+    NO = len(others[0])
+    is_gath = core in gath
+    kk = [k for k in range(ng) if core == gath[k] or core in others[k]]
+    kk = kk[0] if kk else None
+    relays = [grp[2 * x] for grp in groups for x in range(2)]
+    one_from = {far[i]: relays[i] for i in range(nf)}
+    for c in peers:
+        one_from[c] = rootc
+    one_to = [c for c in cores if one_from.get(c) == core]
 
     tot, seen = {}, {}
 
@@ -102,8 +115,8 @@ def rank_program(g, core, T, topo):
         for k, r in enumerate(rel):
             fs = far[2 * k:2 * k + 2]
             plan.append((r, [([fs[i]], _pick(topo.mask(r, fs[i]), 4 * i, 4)) for i in range(len(fs))]))
-            others = [c for c in groups[k] if c != r]
-            plan.append((r, [(others, upper(r, others[0], fs[0]))]))
+            rest = [c for c in groups[k] if c != r]
+            plan.append((r, [(rest, upper(r, rest[0], fs[0]))]))
         return plan
 
     plans = [q_plan(0), q_plan(1)]
@@ -138,32 +151,52 @@ def rank_program(g, core, T, topo):
 
     if is_root:
         inc(Y.dma_start(T.qb[:], T.q[:]), "ldq", 16)
-        wait(Y, "ldq")
-    inc(Y.dma_start(T.kb[:], T.k[:]), "ldk", 16)
-    inc(Y.dma_start(T.vb[:, 0:512], T.v[:]), "ldv", 16)
+        expect("ldk", 16)
+        expect("ldv", 16)
+    else:
+        inc(Y.dma_start(T.kb[:], T.k[:]), "ldk", 16)
+        inc(Y.dma_start(T.vb[:, 0:512], T.v[:]), "ldv", 16)
 
-    inc(V.memset(T.z[:], 0.0), "ms0")
+    if core not in one_from:
+        inc(V.memset(T.vb[:, 512:1024], 1.0), "one")
+        wait(V, "one")
+        inc(V.quantize_mx(T.vc[:, 128:256], T.vs[:, 128:256], T.vb[:, 512:1024]), "qo")
+    inc(V.memset(T.wrow[0:32, :], -1.0), "ms0")
     inc(V.memset(T.one32[:], 1.0), "ms")
     inc(V.memset(T.d1[:], -20.0), "ms")
-    inc(V.memset(T.wrow[0:32, :], 0.0), "ms")
     inc(V.memset(T.wT[:], 0.0), "ms")
+    wait(V, "ms0")
     wait(V, "ms")
-    wait(S, "ms0")
-    inc(S.activation(T.vb[:, 512:1024], T.z[:], AF.Exp), "one")
+    if not is_root:
+        wait(S, "ms0")
+        inc(S.activation(T.wrow[0:32, :], T.wrow[0:32, :], AF.Exp), "w1")
+        wait(Y, "w1")
+        inc(Y.dma_start(T.w[:], T.wrow[0:N, :]), "stw", 16)
     if is_root:
         wait(V, "ldq")
         inc(V.quantize_mx(T.qc[:], T.qs[:], T.qb[:]), "qq")
     inc(V.memset(T.d0[:], -1e29), "ms2")
     wait(V, "ms2")
-    wait(V, "one")
-    inc(V.quantize_mx(T.vc[:, 128:256], T.vs[:, 128:256], T.vb[:, 512:1024]), "qv")
     wait(V, "ldv")
     inc(V.quantize_mx(T.vc[:, 0:128], T.vs[:, 0:128], T.vb[:, 0:512]), "qv")
     wait(V, "ldk")
     inc(V.quantize_mx(T.kc[:], T.ks[:], T.kb[:]), "qk")
-    if not is_root:
-        wait(Y, "ms")
-        inc(Y.dma_start(T.w[:], T.wrow[0:N, :]), "stw", 16)
+
+    if core in one_from:
+        expect("qoa", _cnt(topo.mask(one_from[core], core)))
+    if one_to:
+        m = topo.mask(core, one_to[0])
+        h = _cnt(m) // 2
+        ids = []
+        for d in one_to:
+            rid, pid = topo.addr(d, core)
+            ids.append(DstId(rid=rid, pnc=pid))
+        oc, op = T.vc[:, 128:130].bitcast(dt.uint8), T.vs[:, 128:136]
+        wait(g, "qo")
+        g.remote_dma_fused([RemoteDMATransfer(dst_ids=ids, dma_engine_mask=_pick(m, h * x, h), remote_sem=T.sem.qoa,
+                                              srcs=[ap], dsts=[ap for _ in one_to]) for x, ap in enumerate((oc, op))],
+                           local_sem=T.sem.ls)
+        expect("ls", 2 * h)
 
     if is_root:
         wait(g, "qq")
@@ -171,6 +204,9 @@ def rank_program(g, core, T, topo):
         q_call(1, plans[1][0][1])
         q_call(0, plans[0][1][1])
         q_call(1, plans[1][1][1])
+        wait(Y, "ls")
+        Y.dma_start(T.kb[:], T.k[:]).then_inc(T.sem.ldk, 16)
+        Y.dma_start(T.vb[:, 0:512], T.v[:]).then_inc(T.sem.ldv, 16)
     else:
         for which in range(2):
             mine = [trs for snd, trs in plans[which] if snd == core]
@@ -226,67 +262,30 @@ def rank_program(g, core, T, topo):
 
     wait(P, "pq")
     wait(P, "qv")
+    wait(P, "qoa" if core in one_from else "qo")
     inc(P.matmul_mx(ps[:, 3072:3202], T.pc[:], T.pl[:], T.vc[:, 0:130], T.vs[:, 0:130], True, True), "fm")
     wait(V, "fm")
-    own = T.land[:, SL * rank:SL * rank + W] if is_root else T.rt[:, 0:W]
+    own = T.land[:, SL * rank:SL * rank + W] if is_root else (T.land[:, SL * NO:SL * NO + W] if is_gath else T.rt[:, 0:W])
     inc(V.tensor_copy(own, ps[:, 3072:3072 + W]), "rt")
 
-    wait(Y, "cb")
-    inc(Y.dma_start(T.c[:], T.cb[:, 0:1]), "stc", 16)
-    wait(Y, "pe")
-    inc(Y.dma_start(T.p[:], T.pb[:]), "stp", 16)
+    def store_c_p():
+        wait(Y, "cb")
+        inc(Y.dma_start(T.c[:], T.cb[:, 0:1]), "stc", 16)
+        wait(Y, "pe")
+        inc(Y.dma_start(T.p[:], T.pb[:]), "stp", 16)
 
-    if not is_root:
-        slot = T.land[:, SL * rank:SL * rank + W]
-        if core in far:
-            wait(g, "cb")
-            send(fwd[core], T.fcl[:, 0:1], T.cb[:, 0:1], "fca")
-            wait(g, "rt")
-            send(fwd[core], T.ftl[:, 0:W], T.rt[:, 0:W], "fta")
-        else:
-            wait(g, "cb")
-            send(rootc, T.CL[:, rank:rank + 1], T.cb[:, 0:1], "cea")
-            wait(g, "rt")
-            send(rootc, slot, T.rt[:, 0:W], "t%d" % rank)
-            for f in far:
-                if fwd[f] == core:
-                    j = T.rank_of(f)
-                    expect("fca", _cnt(topo.mask(f, core)))
-                    expect("fta", _cnt(topo.mask(f, core)))
-                    wait(g, "fca")
-                    send(rootc, T.CL[:, j:j + 1], T.fcl[:, 0:1], "cla")
-                    wait(g, "fta")
-                    send(rootc, T.land[:, SL * j:SL * j + W], T.ftl[:, 0:W], "t%d" % j)
+    if is_root or is_gath:
+        store_c_p()
 
-    if is_root:
-        for c in peers + mid:
-            expect("cea", _cnt(topo.mask(c, rootc)))
-            expect("t%d" % T.rank_of(c), _cnt(topo.mask(c, rootc)))
-        for f in far:
-            expect("cla", _cnt(topo.mask(fwd[f], rootc)))
-            expect("t%d" % T.rank_of(f), _cnt(topo.mask(fwd[f], rootc)))
-        sm, acc = T.sm, T.acc[:, 0:W]
+    sm, acc = T.sm, T.acc[:, 0:W]
 
-        def slot_of(j):
-            return T.land[:, SL * j:SL * j + W]
+    def slot_of(j):
+        return T.land[:, SL * j:SL * j + W]
 
-        wait(V, "cea")
-        inc(V.tensor_copy(T.CL[:, rank:rank + 1], T.cb[:, 0:1]), "e1")
-        wait(V, "e1")
-        inc(V.tensor_reduce(sm[:, 0:1], T.CL[:, nf:N], AX.X, OP.max), "e2")
-        wait(V, "e2")
-        inc(V.tensor_scalar(sm[:, 1:2], sm[:, 0:1], -1.0, None, OP.mult), "e3")
-        wait(S, "cea")
-        wait(S, "e1")
-        wait(S, "e3")
-        inc(S.activation(T.wp[:, nf:N], T.CL[:, nf:N], AF.Exp, bias=sm[:, 1:2]), "e4")
-        wait(S, "e4")
-        order = [rank] + [T.rank_of(c) for c in peers]
-        for x in (0, 2, 1, 3):
-            order += [T.rank_of(grp[x]) for grp in groups]
+    def weigh_and_add(order, wcol, mine):
         for j in order:
-            wait(S, "rt" if j == rank else "t%d" % j)
-            inc(S.activation(slot_of(j), slot_of(j), AF.Copy, scale=T.wp[:, j:j + 1]), "m%d" % j)
+            wait(S, "rt" if j == mine else "t%d" % j)
+            inc(S.activation(slot_of(j), slot_of(j), AF.Copy, scale=wcol(j)), "m%d" % j)
         for i, j in enumerate(order):
             wait(V, "m%d" % j)
             if i == 1:
@@ -295,46 +294,119 @@ def rank_program(g, core, T, topo):
                 wait(V, "ac")
                 inc(V.tensor_tensor(acc, acc, slot_of(j), OP.add), "ac")
 
+    if not is_root and not is_gath:
+        dst, col = (rootc, rank) if core in peers else (gath[kk], others[kk].index(core))
+        wait(g, "cb")
+        send(dst, T.CL[:, col:col + 1], T.cb[:, 0:1], "cea")
+        wait(g, "rt")
+        send(dst, slot_of(col), T.rt[:, 0:W], "t%d" % col)
+        wait(Y, "ls")
+        store_c_p()
+
+    if is_gath:
+        for i, c in enumerate(others[kk]):
+            expect("cea", _cnt(topo.mask(c, core)))
+            expect("t%d" % i, _cnt(topo.mask(c, core)))
+        wait(g, "cb")
+        send(rootc, T.GT[:, 8 * kk + NO:8 * kk + NO + 1], T.cb[:, 0:1], "cla")
+        wait(g, "cea")
+        send(rootc, T.GT[:, 8 * kk:8 * kk + NO], T.CL[:, 0:NO], "cla")
+        wait(V, "cea")
+        inc(V.tensor_reduce(sm[:, 0:1], T.CL[:, 0:NO], AX.X, OP.max), "e2")
+        wait(V, "e2")
+        inc(V.tensor_scalar(sm[:, 1:2], sm[:, 0:1], T.cb[:, 0:1], -1.0, OP.max, OP.mult), "e3")
+        wait(S, "cea")
+        wait(S, "cb")
+        wait(S, "e3")
+        inc(S.activation(T.wp[:, 0:NO], T.CL[:, 0:NO], AF.Exp, bias=sm[:, 1:2]), "e4")
+        inc(S.activation(T.wp[:, NO:NO + 1], T.cb[:, 0:1], AF.Exp, bias=sm[:, 1:2]), "e4")
+        wait(S, "e4")
+        nfk = len(farm[kk])
+        weigh_and_add([NO] + list(range(nfk, NO)) + list(range(nfk)), lambda j: T.wp[:, j:j + 1], NO)
+        wait(g, "ac")
+        send(rootc, slot_of(rank), acc, "t%d" % rank)
+
+    if is_root:
+        rr = sorted(T.rank_of(c) for c in peers + [rootc])
+        lo, hi = rr[0], rr[-1] + 1
+        for c in peers:
+            expect("cea", _cnt(topo.mask(c, rootc)))
+            expect("t%d" % T.rank_of(c), _cnt(topo.mask(c, rootc)))
+        for c in gath:
+            expect("cla", 2 * _cnt(topo.mask(c, rootc)))
+            expect("t%d" % T.rank_of(c), _cnt(topo.mask(c, rootc)))
+
+        wait(V, "cea")
+        inc(V.tensor_copy(T.CL[:, rank:rank + 1], T.cb[:, 0:1]), "e1")
+        wait(V, "e1")
+        inc(V.tensor_reduce(sm[:, 0:1], T.CL[:, lo:hi], AX.X, OP.max), "e2")
+        wait(V, "e2")
+        inc(V.tensor_scalar(sm[:, 4:5], sm[:, 0:1], -1.0, None, OP.mult), "e3")
+        wait(S, "cea")
+        wait(S, "e1")
+        wait(S, "e3")
+        inc(S.activation(T.wp[:, lo:hi], T.CL[:, lo:hi], AF.Exp, bias=sm[:, 4:5]), "e4")
+        wait(S, "e4")
+        weigh_and_add([rank] + [T.rank_of(c) for c in peers], lambda j: T.wp[:, j:j + 1], rank)
+
         wait(V, "cla")
-        inc(V.tensor_reduce(sm[:, 2:3], T.CL[:, 0:nf], AX.X, OP.max), "f1")
+        for k in range(ng):
+            inc(V.tensor_reduce(sm[:, 1 + k:2 + k], T.GT[:, 8 * k:8 * k + NO + 1], AX.X, OP.max), "f1")
         wait(V, "f1")
-        inc(V.tensor_scalar(sm[:, 3:4], sm[:, 2:3], sm[:, 0:1], -1.0, OP.max, OP.mult), "f2")
+        inc(V.tensor_reduce(sm[:, 3:4], sm[:, 0:1 + ng], AX.X, OP.max, negate=True), "f2")
+        inc(V.tensor_scalar(sm[:, 5:5 + ng], sm[:, 1:1 + ng], -1.0, None, OP.mult), "f2")
         wait(S, "cla")
         wait(S, "f2")
-        inc(S.activation(sm[:, 4:5], sm[:, 0:1], AF.Exp, bias=sm[:, 3:4]), "f3")
-        inc(S.activation(T.wT[:, 0:nf], T.CL[:, 0:nf], AF.Exp, bias=sm[:, 3:4]), "f4")
+        inc(S.activation(sm[:, 8:9 + ng], sm[:, 0:1 + ng], AF.Exp, bias=sm[:, 3:4]), "f3")
+        for k in range(ng):
+            inc(S.activation(T.wg[:, 8 * k:8 * k + NO + 1], T.GT[:, 8 * k:8 * k + NO + 1], AF.Exp, bias=sm[:, 5 + k:6 + k]),
+                "f4")
         wait(V, "f3")
         wait(V, "ac")
-        inc(V.tensor_scalar(acc, acc, sm[:, 4:5], None, OP.mult), "ac")
-        wait(V, "e4")
-        inc(V.tensor_scalar(T.wT[:, nf:N], T.wp[:, nf:N], sm[:, 4:5], None, OP.mult), "f5")
-        wait(V, "f4")
+        inc(V.tensor_scalar(acc, acc, sm[:, 8:9], None, OP.mult), "ac")
+        wait(S, "f3")
+        wait(S, "f4")
+        inc(S.activation(T.wT[:, lo:hi], T.wp[:, lo:hi], AF.Copy, scale=sm[:, 8:9]), "f5")
+        for k in range(ng):
+            F = sm[:, 9 + k:10 + k]
+            for i, c in enumerate(farm[k]):
+                j = T.rank_of(c)
+                inc(S.activation(T.wT[:, j:j + 1], T.wg[:, 8 * k + i:8 * k + i + 1], AF.Copy, scale=F), "f5")
+            g0, n, x = T.rank_of(groups[k][0]), len(groups[k]), 8 * k + len(farm[k])
+            inc(S.activation(T.wT[:, g0:g0 + n], T.wg[:, x:x + n], AF.Copy, scale=F), "f5")
         wait(V, "f5")
         for a in range(4):
             inc(V.transpose(T.wrow[0:32, 32 * a:32 * a + 32], T.wT[32 * a:32 * a + 32, :]), "wt")
         wait(Y, "wt")
         inc(Y.dma_start(T.w[:], T.wrow[0:N, :]), "stw", 16)
 
-        wait(S, "f4")
-        for j in range(nf):
+        for k in range(ng):
+            j = T.rank_of(gath[k])
             wait(S, "t%d" % j)
-            inc(S.activation(slot_of(j), slot_of(j), AF.Copy, scale=T.wT[:, j:j + 1]), "m%d" % j)
-        for j in range(nf):
-            wait(V, "m%d" % j)
+            inc(S.activation(slot_of(j), slot_of(j), AF.Copy, scale=sm[:, 9 + k:10 + k]), "m%d" % j)
+        for k in range(ng):
+            wait(V, "m%d" % T.rank_of(gath[k]))
             wait(V, "ac")
-            inc(V.tensor_tensor(acc, acc, slot_of(j), OP.add), "ac")
+            inc(V.tensor_tensor(acc, acc, slot_of(T.rank_of(gath[k])), OP.add), "ac")
 
         wait(V, "ac")
-        inc(V.reciprocal(sm[:, 5:6], T.acc[:, 128:129]), "rd")
+        inc(V.reciprocal(sm[:, 12:13], T.acc[:, 128:129]), "rd")
         wait(V, "rd")
-        inc(V.tensor_scalar(T.X[:], T.acc[:, 0:128], sm[:, 5:6], None, OP.mult), "xx")
+        inc(V.tensor_scalar(T.X[:], T.acc[:, 0:128], sm[:, 12:13], None, OP.mult), "xx")
         wait(V, "xx")
+        inc(V.transpose(T.X2[:], T.X[:]), "xt")
+        wait(V, "xt")
+        wait(S, "xt")
         for b in range(4):
             for a in range(4):
-                inc(V.transpose(T.Z[32 * b:32 * b + 32, 32 * a:32 * a + 32], T.X[32 * a:32 * a + 32, 32 * b:32 * b + 32]),
-                    "z%d" % b)
+                dst_ap = T.Z[32 * b:32 * b + 32, 32 * a:32 * a + 32]
+                src_ap = T.X2[32 * a:32 * a + 32, 32 * b:32 * b + 32]
+                if a % 2 == 0:
+                    inc(V.tensor_copy(dst_ap, src_ap), "z%d" % b)
+                else:
+                    inc(S.activation(dst_ap, src_ap, AF.Copy), "z%d" % b)
         for b in range(4):
-            q = Y if b % 2 == 0 else S
+            q = Y if b < 3 else S
             wait(q, "z%d" % b)
             inc(q.dma_start(T.o[32 * b:32 * b + 32, :], T.Z[32 * b:32 * b + 32, :]), "sto", 16)
 

import numpy as np
from concourse.bass import DstId, RemoteDMATransfer
from concourse.mybir import dt, AluOpType, AxisListType, ActivationFunctionType

N = 16
W = 129
SL = 132
A = float(np.float32(0.0125))

SCRATCH = {
    "qb": ("sbuf", [128, 512], "bfloat16"),
    "qc": ("sbuf", [128, 128], "float8_e4m3fn_x4"),
    "qs": ("sbuf", [128, 128], "uint8"),
    "kb": ("sbuf", [128, 2048], "bfloat16"),
    "kc": ("sbuf", [128, 512], "float8_e4m3fn_x4"),
    "ks": ("sbuf", [128, 512], "uint8"),
    "vb": ("sbuf", [128, 1024], "bfloat16"),
    "vc": ("sbuf", [128, 256], "float8_e4m3fn_x4"),
    "vs": ("sbuf", [128, 256], "uint8"),
    "one32": ("sbuf", [128, 32], "float32"),
    "m2": ("sbuf", [128, 4], "float32"),
    "cb": ("sbuf", [128, 32], "float32"),
    "d0": ("sbuf", [128, 1024], "float32"),
    "d1": ("sbuf", [128, 256], "float32"),
    "d2": ("sbuf", [128, 1024], "float32"),
    "pb": ("sbuf", [128, 512], "bfloat16"),
    "pc": ("sbuf", [128, 128], "float8_e4m3fn_x4"),
    "pl": ("sbuf", [128, 128], "uint8"),
    "rt": ("sbuf", [128, SL], "float32"),
    "land": ("sbuf", [128, N * SL], "float32"),
    "CL": ("sbuf", [128, N], "float32"),
    "GT": ("sbuf", [128, 16], "float32"),
    "wg": ("sbuf", [128, 16], "float32"),
    "sm": ("sbuf", [128, 16], "float32"),
    "wp": ("sbuf", [128, N], "float32"),
    "wT": ("sbuf", [128, 32], "float32"),
    "wrow": ("sbuf", [128, 128], "float32"),
    "acc": ("sbuf", [128, SL], "float32"),
    "X": ("sbuf", [128, 128], "float32"),
    "X2": ("sbuf", [128, 128], "float32"),
    "Z": ("sbuf", [128, 128], "float32"),
    "ps": ("psum", [128, 3584], "float32"),
}
SEMAPHORES = (["ldq", "ldk", "ldv", "stc", "stp", "stw", "sto", "ms0", "ms", "ms2", "one", "w1", "qo", "qoa", "qq", "qv",
               "qk", "qca", "qsa",
               "st1", "st2", "r", "cm", "cb", "tr", "cp", "pe", "pq", "fm", "rt", "ls", "cea", "cla", "xt",
               "e1", "e2", "e3", "e4", "ac", "f1", "f2", "f3", "f4", "f5", "wt", "rd", "xx"]
              + ["s%d" % b for b in range(4)] + ["u%d" % b for b in range(4)] + ["sc%d" % b for b in range(4)]
              + ["z%d" % b for b in range(4)] + ["t%d" % j for j in range(N)] + ["m%d" % j for j in range(N)])


def _cnt(mask):
    return bin(mask).count("1")


def _pick(mask, lo, n):
    bits = [b for b in range(16) if (mask >> b) & 1]
    return sum(1 << b for b in bits[lo:lo + n])


def rank_program(g, core, T, topo):
    rank = T.rank_of(core)
    if rank is None:
        return
    V, S, P, Y = g.vector, g.scalar, g.tensor, g.sync
    AF, OP, AX = ActivationFunctionType, AluOpType, AxisListType
    cores = list(T.cores)
    rootc = cores[T.root]
    is_root = core == rootc

    def samechip(a, b):
        return topo.host(a) == topo.host(b) and topo.chip(a) == topo.chip(b)

    far = [c for c in cores if c != rootc and not topo.may_write(c, rootc)]
    peers = [c for c in cores if c != rootc and samechip(c, rootc)]
    mid = [c for c in cores if c != rootc and c not in far and c not in peers]
    groups = [[c for c in mid if topo.host(c) == h] for h in sorted(set(topo.host(c) for c in mid))]
    nf = len(far)
    ng = len(groups)
    gath = [grp[-1] for grp in groups]
    farm = [[far[i] for i in range(nf) if i % ng == k] for k in range(ng)]
    others = [farm[k] + groups[k][:-1] for k in range(ng)]
    NO = len(others[0])
    is_gath = core in gath
    kk = [k for k in range(ng) if core == gath[k] or core in others[k]]
    kk = kk[0] if kk else None
    relays = [grp[2 * x] for grp in groups for x in range(2)]
    one_from = {far[i]: relays[i] for i in range(nf)}
    for c in peers:
        one_from[c] = rootc
    one_to = [c for c in cores if one_from.get(c) == core]

    tot, seen = {}, {}

    def inc(ins, name, n=1):
        ins.then_inc(T.sem[name], n)
        tot[name] = tot.get(name, 0) + n

    def expect(name, n):
        tot[name] = tot.get(name, 0) + n

    def wait(q, name):
        q.wait_ge(T.sem[name], tot[name])
        seen[name] = tot[name]

    def upper(src, on_dst, off_dst):
        on = topo.mask(src, on_dst)
        up = on & ~topo.mask(src, off_dst)
        return up if up else on

    def q_plan(which):
        rel = [grp[2 * which] for grp in groups]
        plan = [(rootc, [([rel[k]], _pick(topo.mask(rootc, rel[k]), 4 * k, 4)) for k in range(len(groups))]),
                (rootc, [(peers, upper(rootc, peers[0], rel[0]))])]
        for k, r in enumerate(rel):
            fs = far[2 * k:2 * k + 2]
            plan.append((r, [([fs[i]], _pick(topo.mask(r, fs[i]), 4 * i, 4)) for i in range(len(fs))]))
            rest = [c for c in groups[k] if c != r]
            plan.append((r, [(rest, upper(r, rest[0], fs[0]))]))
        return plan

    plans = [q_plan(0), q_plan(1)]
    qsem = ["qca", "qsa"]
    for which in range(2):
        for snd, trs in plans[which]:
            for dsts, m in trs:
                if core in dsts:
                    expect(qsem[which], _cnt(m))

    def q_ap(which):
        return T.qc[:].bitcast(dt.uint8) if which == 0 else T.qs[:]

    def q_call(which, trs):
        lst = []
        for dsts, m in trs:
            ids = []
            for d in dsts:
                rid, pid = topo.addr(d, core)
                ids.append(DstId(rid=rid, pnc=pid))
            lst.append(RemoteDMATransfer(dst_ids=ids, dma_engine_mask=m, remote_sem=T.sem[qsem[which]],
                                         srcs=[q_ap(which)], dsts=[q_ap(which) for _ in dsts]))
            expect("ls", _cnt(m))
        g.remote_dma_fused(lst, local_sem=T.sem.ls)

    def send(dst, out_ap, in_ap, sem):
        rid, pid = topo.addr(dst, core)
        m = topo.mask(core, dst)
        g.remote_dma(out_ap=out_ap, in_ap=in_ap, remote_sem=T.sem[sem], local_sem=T.sem.ls, pid=pid, routing_id=rid,
                     dma_engine_mask=m)
        expect("ls", _cnt(m))

    if is_root:
        inc(Y.dma_start(T.qb[:], T.q[:]), "ldq", 16)
        expect("ldk", 16)
        expect("ldv", 16)
    else:
        inc(Y.dma_start(T.kb[:], T.k[:]), "ldk", 16)
        inc(Y.dma_start(T.vb[:, 0:512], T.v[:]), "ldv", 16)

    if core not in one_from:
        inc(V.memset(T.vb[:, 512:1024], 1.0), "one")
        wait(V, "one")
        inc(V.quantize_mx(T.vc[:, 128:256], T.vs[:, 128:256], T.vb[:, 512:1024]), "qo")
    inc(V.memset(T.wrow[0:32, :], -1.0), "ms0")
    inc(V.memset(T.one32[:], 1.0), "ms")
    inc(V.memset(T.d1[:], -20.0), "ms")
    inc(V.memset(T.wT[:], 0.0), "ms")
    wait(V, "ms0")
    wait(V, "ms")
    if not is_root:
        wait(S, "ms0")
        inc(S.activation(T.wrow[0:32, :], T.wrow[0:32, :], AF.Exp), "w1")
        wait(Y, "w1")
        inc(Y.dma_start(T.w[:], T.wrow[0:N, :]), "stw", 16)
    if is_root:
        wait(V, "ldq")
        inc(V.quantize_mx(T.qc[:], T.qs[:], T.qb[:]), "qq")
    inc(V.memset(T.d0[:], -1e29), "ms2")
    wait(V, "ms2")
    wait(V, "ldv")
    inc(V.quantize_mx(T.vc[:, 0:128], T.vs[:, 0:128], T.vb[:, 0:512]), "qv")
    wait(V, "ldk")
    inc(V.quantize_mx(T.kc[:], T.ks[:], T.kb[:]), "qk")

    if core in one_from:
        expect("qoa", _cnt(topo.mask(one_from[core], core)))
    if one_to:
        m = topo.mask(core, one_to[0])
        h = _cnt(m) // 2
        ids = []
        for d in one_to:
            rid, pid = topo.addr(d, core)
            ids.append(DstId(rid=rid, pnc=pid))
        oc, op = T.vc[:, 128:130].bitcast(dt.uint8), T.vs[:, 128:136]
        wait(g, "qo")
        g.remote_dma_fused([RemoteDMATransfer(dst_ids=ids, dma_engine_mask=_pick(m, h * x, h), remote_sem=T.sem.qoa,
                                              srcs=[ap], dsts=[ap for _ in one_to]) for x, ap in enumerate((oc, op))],
                           local_sem=T.sem.ls)
        expect("ls", 2 * h)

    if is_root:
        wait(g, "qq")
        q_call(0, plans[0][0][1])
        q_call(1, plans[1][0][1])
        q_call(0, plans[0][1][1])
        q_call(1, plans[1][1][1])
        wait(Y, "ls")
        Y.dma_start(T.kb[:], T.k[:]).then_inc(T.sem.ldk, 16)
        Y.dma_start(T.vb[:, 0:512], T.v[:]).then_inc(T.sem.ldv, 16)
    else:
        for which in range(2):
            mine = [trs for snd, trs in plans[which] if snd == core]
            if mine:
                wait(g, qsem[which])
                for trs in mine:
                    q_call(which, trs)

    ps = T.ps
    wait(P, "qk")
    if is_root:
        wait(P, "qq")
    else:
        wait(P, "qca")
        wait(P, "qsa")
    inc(P.matmul_mx(ps[:, 0:256], T.qc[:], T.qs[:], T.kc[:, 0:256], T.ks[:, 0:256], True, True), "st1")
    inc(P.matmul_mx(ps[:, 512:768], T.qc[:], T.qs[:], T.kc[:, 256:512], T.ks[:, 256:512], True, True), "st2")
    for b in range(4):
        inc(P.matmul_mx(ps[:, 1024 + 512 * b:1152 + 512 * b], T.kc[:, 128 * b:128 * b + 128],
                        T.ks[:, 128 * b:128 * b + 128], T.qc[:], T.qs[:], True, True), "s%d" % b)

    wait(V, "st1")
    inc(V.tensor_reduce(T.m2[:, 0:1], ps[:, 0:256], AX.X, OP.max), "r")
    wait(V, "st2")
    inc(V.tensor_reduce(T.m2[:, 1:2], ps[:, 512:768], AX.X, OP.max), "r")
    wait(V, "r")
    inc(V.tensor_scalar(T.m2[:, 2:3], T.m2[:, 0:1], T.m2[:, 1:2], A, OP.max, OP.mult), "cm")
    wait(V, "cm")
    inc(V.tensor_scalar(T.cb[:], T.one32[:], T.m2[:, 2:3], None, OP.mult), "cb")
    wait(V, "cb")
    for a in range(4):
        inc(V.transpose(T.d1[0:32, 64 * a:64 * a + 64:2], T.cb[32 * a:32 * a + 32, :]), "tr")
    wait(V, "tr")
    inc(V.tensor_copy(T.d1[32:64, 0:256:2], T.d1[0:32, 0:256:2]), "cp")
    wait(V, "cp")
    inc(V.tensor_copy(T.d1[64:128, 0:256:2], T.d1[0:64, 0:256:2]), "cp")
    wait(V, "cp")

    wait(S, "ms2")
    for b in range(4):
        wait(S, "s%d" % b)
        inc(S.activation(T.d0[:, 256 * b + 1:256 * b + 256:2], ps[:, 1024 + 512 * b:1152 + 512 * b], AF.Copy, scale=A),
            "u%d" % b)
    for b in range(4):
        wait(V, "u%d" % b)
        inc(V.tensor_tensor_scan(T.d2[:, 256 * b:256 * b + 256], T.d0[:, 256 * b:256 * b + 256], T.d1[:], 0.0,
                                 OP.subtract, OP.max), "sc%d" % b)
    for b in range(4):
        wait(S, "sc%d" % b)
        inc(S.activation(T.pb[:, b:512:4], T.d2[:, 256 * b + 1:256 * b + 256:2], AF.Exp), "pe")
    wait(V, "pe")
    inc(V.quantize_mx(T.pc[:], T.pl[:], T.pb[:]), "pq")

    wait(P, "pq")
    wait(P, "qv")
    wait(P, "qoa" if core in one_from else "qo")
    inc(P.matmul_mx(ps[:, 3072:3202], T.pc[:], T.pl[:], T.vc[:, 0:130], T.vs[:, 0:130], True, True), "fm")
    wait(V, "fm")
    own = T.land[:, SL * rank:SL * rank + W] if is_root else (T.land[:, SL * NO:SL * NO + W] if is_gath else T.rt[:, 0:W])
    inc(V.tensor_copy(own, ps[:, 3072:3072 + W]), "rt")

    def store_c_p():
        wait(Y, "cb")
        inc(Y.dma_start(T.c[:], T.cb[:, 0:1]), "stc", 16)
        wait(Y, "pe")
        inc(Y.dma_start(T.p[:], T.pb[:]), "stp", 16)

    if is_root or is_gath:
        store_c_p()

    sm, acc = T.sm, T.acc[:, 0:W]

    def slot_of(j):
        return T.land[:, SL * j:SL * j + W]

    def weigh_and_add(order, wcol, mine):
        for j in order:
            wait(S, "rt" if j == mine else "t%d" % j)
            inc(S.activation(slot_of(j), slot_of(j), AF.Copy, scale=wcol(j)), "m%d" % j)
        for i, j in enumerate(order):
            wait(V, "m%d" % j)
            if i == 1:
                inc(V.tensor_tensor(acc, slot_of(order[0]), slot_of(j), OP.add), "ac")
            elif i > 1:
                wait(V, "ac")
                inc(V.tensor_tensor(acc, acc, slot_of(j), OP.add), "ac")

    if not is_root and not is_gath:
        dst, col = (rootc, rank) if core in peers else (gath[kk], others[kk].index(core))
        wait(g, "cb")
        send(dst, T.CL[:, col:col + 1], T.cb[:, 0:1], "cea")
        wait(g, "rt")
        send(dst, slot_of(col), T.rt[:, 0:W], "t%d" % col)
        wait(Y, "ls")
        store_c_p()

    if is_gath:
        for i, c in enumerate(others[kk]):
            expect("cea", _cnt(topo.mask(c, core)))
            expect("t%d" % i, _cnt(topo.mask(c, core)))
        wait(g, "cb")
        send(rootc, T.GT[:, 8 * kk + NO:8 * kk + NO + 1], T.cb[:, 0:1], "cla")
        wait(g, "cea")
        send(rootc, T.GT[:, 8 * kk:8 * kk + NO], T.CL[:, 0:NO], "cla")
        wait(V, "cea")
        inc(V.tensor_reduce(sm[:, 0:1], T.CL[:, 0:NO], AX.X, OP.max), "e2")
        wait(V, "e2")
        inc(V.tensor_scalar(sm[:, 1:2], sm[:, 0:1], T.cb[:, 0:1], -1.0, OP.max, OP.mult), "e3")
        wait(S, "cea")
        wait(S, "cb")
        wait(S, "e3")
        inc(S.activation(T.wp[:, 0:NO], T.CL[:, 0:NO], AF.Exp, bias=sm[:, 1:2]), "e4")
        inc(S.activation(T.wp[:, NO:NO + 1], T.cb[:, 0:1], AF.Exp, bias=sm[:, 1:2]), "e4")
        wait(S, "e4")
        nfk = len(farm[kk])
        weigh_and_add([NO] + list(range(nfk, NO)) + list(range(nfk)), lambda j: T.wp[:, j:j + 1], NO)
        wait(g, "ac")
        send(rootc, slot_of(rank), acc, "t%d" % rank)

    if is_root:
        rr = sorted(T.rank_of(c) for c in peers + [rootc])
        lo, hi = rr[0], rr[-1] + 1
        for c in peers:
            expect("cea", _cnt(topo.mask(c, rootc)))
            expect("t%d" % T.rank_of(c), _cnt(topo.mask(c, rootc)))
        for c in gath:
            expect("cla", 2 * _cnt(topo.mask(c, rootc)))
            expect("t%d" % T.rank_of(c), _cnt(topo.mask(c, rootc)))

        wait(V, "cea")
        inc(V.tensor_copy(T.CL[:, rank:rank + 1], T.cb[:, 0:1]), "e1")
        wait(V, "e1")
        inc(V.tensor_reduce(sm[:, 0:1], T.CL[:, lo:hi], AX.X, OP.max), "e2")
        wait(V, "e2")
        inc(V.tensor_scalar(sm[:, 4:5], sm[:, 0:1], -1.0, None, OP.mult), "e3")
        wait(S, "cea")
        wait(S, "e1")
        wait(S, "e3")
        inc(S.activation(T.wp[:, lo:hi], T.CL[:, lo:hi], AF.Exp, bias=sm[:, 4:5]), "e4")
        wait(S, "e4")
        weigh_and_add([rank] + [T.rank_of(c) for c in peers], lambda j: T.wp[:, j:j + 1], rank)

        wait(V, "cla")
        for k in range(ng):
            inc(V.tensor_reduce(sm[:, 1 + k:2 + k], T.GT[:, 8 * k:8 * k + NO + 1], AX.X, OP.max), "f1")
        wait(V, "f1")
        inc(V.tensor_reduce(sm[:, 3:4], sm[:, 0:1 + ng], AX.X, OP.max, negate=True), "f2")
        inc(V.tensor_scalar(sm[:, 5:5 + ng], sm[:, 1:1 + ng], -1.0, None, OP.mult), "f2")
        wait(S, "cla")
        wait(S, "f2")
        inc(S.activation(sm[:, 8:9 + ng], sm[:, 0:1 + ng], AF.Exp, bias=sm[:, 3:4]), "f3")
        for k in range(ng):
            inc(S.activation(T.wg[:, 8 * k:8 * k + NO + 1], T.GT[:, 8 * k:8 * k + NO + 1], AF.Exp, bias=sm[:, 5 + k:6 + k]),
                "f4")
        wait(V, "f3")
        wait(V, "ac")
        inc(V.tensor_scalar(acc, acc, sm[:, 8:9], None, OP.mult), "ac")
        wait(S, "f3")
        wait(S, "f4")
        inc(S.activation(T.wT[:, lo:hi], T.wp[:, lo:hi], AF.Copy, scale=sm[:, 8:9]), "f5")
        for k in range(ng):
            F = sm[:, 9 + k:10 + k]
            for i, c in enumerate(farm[k]):
                j = T.rank_of(c)
                inc(S.activation(T.wT[:, j:j + 1], T.wg[:, 8 * k + i:8 * k + i + 1], AF.Copy, scale=F), "f5")
            g0, n, x = T.rank_of(groups[k][0]), len(groups[k]), 8 * k + len(farm[k])
            inc(S.activation(T.wT[:, g0:g0 + n], T.wg[:, x:x + n], AF.Copy, scale=F), "f5")
        wait(V, "f5")
        for a in range(4):
            inc(V.transpose(T.wrow[0:32, 32 * a:32 * a + 32], T.wT[32 * a:32 * a + 32, :]), "wt")
        wait(Y, "wt")
        inc(Y.dma_start(T.w[:], T.wrow[0:N, :]), "stw", 16)

        for k in range(ng):
            j = T.rank_of(gath[k])
            wait(S, "t%d" % j)
            inc(S.activation(slot_of(j), slot_of(j), AF.Copy, scale=sm[:, 9 + k:10 + k]), "m%d" % j)
        for k in range(ng):
            wait(V, "m%d" % T.rank_of(gath[k]))
            wait(V, "ac")
            inc(V.tensor_tensor(acc, acc, slot_of(T.rank_of(gath[k])), OP.add), "ac")

        wait(V, "ac")
        inc(V.reciprocal(sm[:, 12:13], T.acc[:, 128:129]), "rd")
        wait(V, "rd")
        inc(V.tensor_scalar(T.X[:], T.acc[:, 0:128], sm[:, 12:13], None, OP.mult), "xx")
        wait(V, "xx")
        inc(V.transpose(T.X2[:], T.X[:]), "xt")
        wait(V, "xt")
        wait(S, "xt")
        for b in range(4):
            for a in range(4):
                dst_ap = T.Z[32 * b:32 * b + 32, 32 * a:32 * a + 32]
                src_ap = T.X2[32 * a:32 * a + 32, 32 * b:32 * b + 32]
                if a % 2 == 0:
                    inc(V.tensor_copy(dst_ap, src_ap), "z%d" % b)
                else:
                    inc(S.activation(dst_ap, src_ap, AF.Copy), "z%d" % b)
        for b in range(4):
            q = Y if b < 3 else S
            wait(q, "z%d" % b)
            inc(q.dma_start(T.o[32 * b:32 * b + 32, :], T.Z[32 * b:32 * b + 32, :]), "sto", 16)

    for name in sorted(tot):
        if seen.get(name, 0) < tot[name]:
            wait(g, name)
